import numpy as np
import ml_dtypes


def mxq(x, axis, fmt="e4m3"):
    dtype, down = {"e4m3": (ml_dtypes.float8_e4m3fn, 7), "e5m2": (ml_dtypes.float8_e5m2, 14)}[fmt]
    v = np.moveaxis(np.asarray(x, np.float32).astype(ml_dtypes.bfloat16).astype(np.float64), axis, -1)
    blocks = v.reshape(v.shape[:-1] + (-1, 32))
    amax = np.abs(blocks).max(-1, keepdims=True)
    byte = np.maximum(np.where(amax > 0, np.frexp(amax)[1] - 1 + 127, 0) - down, 1)
    scale = np.exp2(byte - 127.0)
    codes = (blocks / scale).astype(np.float32).astype(dtype).astype(np.float64)
    return np.moveaxis((codes * scale).reshape(v.shape), -1, axis)


WIDE = False


def mx_kscale(k):
    if not WIDE:
        return np.ones(k)
    levels = np.array([10, -10, 5, -5, 0])
    if k % 512:
        return np.exp2(np.random.permutation(np.resize(levels, k // 32))).repeat(32)
    a = np.empty((k // 512, 16))
    for p in range(k // 512):
        a[p, :8] = np.random.permutation(np.resize(levels, 8))
        for g in range(8):
            far = levels[np.abs(levels - a[p, g]) >= 10]
            a[p, g + 8] = far[np.random.randint(len(far))]
    return np.exp2(a.ravel()).repeat(32)


def f64(x):
    return np.asarray(x).astype(np.float64)


def striped(idx):
    return np.tile(np.asarray(idx).reshape(-1, 16).T, (8, 1)).astype(np.uint16)


def unstriped(offs):
    return offs[:16].T.reshape(-1).astype(np.int64)


E2M1 = np.array([0.0, 0.5, 1.0, 1.5, 2.0, 3.0, 4.0, 6.0, -0.0, -0.5, -1.0, -1.5, -2.0, -3.0, -4.0, -6.0])


def pack_weight(w, fmt):
    k, n = w.shape
    w = f64(np.asarray(w, np.float32).astype(ml_dtypes.bfloat16)).reshape(k // 32, 32, n)
    amax = np.abs(w).max(1)
    if fmt == "e4m3":
        byte = np.frexp(amax)[1] - 1 + 127 - 7
    else:
        mant, ex = np.frexp(amax / 6.0)
        byte = np.where(mant > 0.5, ex, ex - 1) + 127
    byte = np.clip(np.where(amax > 0, byte, 1), 1, 254)
    scaled = (w * np.exp2(127.0 - byte)[:, None, :]).reshape(k, n).astype(np.float32)
    by_word = np.ascontiguousarray(scaled.reshape(k // 512, 128, 4, n).transpose(0, 1, 3, 2))
    if fmt == "e4m3":
        words = by_word.astype(ml_dtypes.float8_e4m3fn).view(np.uint8)
    else:
        c = by_word.astype(ml_dtypes.float4_e2m1fn).view(np.uint8) & 0xF
        words = (c[..., 0::2] | (c[..., 1::2] << 4)).reshape(k // 512, 128, 2 * n)
    return np.ascontiguousarray(words), np.ascontiguousarray(byte.astype(np.uint8).reshape(k // 512, 16, n))


def unpack_weight(words, scales, fmt):
    g, _, n = scales.shape
    words = np.ascontiguousarray(words).reshape(g, 128, n, -1)
    if fmt == "e4m3":
        vals = words.view(ml_dtypes.float8_e4m3fn).astype(np.float64)
    else:
        nib = np.empty((g, 128, n, 4), np.uint8)
        nib[..., 0::2] = words & 0xF
        nib[..., 1::2] = words >> 4
        vals = E2M1[nib]
    vals = vals * np.repeat(np.exp2(scales.astype(np.float64) - 127.0), 8, axis=1)[..., None]
    return vals.transpose(0, 1, 3, 2).reshape(g * 512, n)


def bf(x):
    return np.asarray(x, np.float32).astype(ml_dtypes.bfloat16)


def planes(Y):
    r, m = Y.shape
    b = f64(bf(Y)).reshape(r // 32, 32, m)
    amax = np.abs(b).max(1)
    byte = np.clip(np.where(amax > 0, np.frexp(amax)[1] - 1 + 127 - 7, 1), 1, 254)
    codes = (b * np.exp2(127.0 - byte)[:, None, :]).reshape(r, m).astype(np.float32).astype(ml_dtypes.float8_e4m3fn).view(np.uint8)
    words = codes.reshape(r // 512, 128, 4, m).transpose(0, 1, 3, 2)
    return np.ascontiguousarray(words), np.ascontiguousarray(byte.astype(np.uint8).reshape(r // 512, 16, m))


D, T, I, Q, E, Z = 512, 2048, 512, 256, 512, 1024


def setup_inputs():
    n = np.random.standard_normal
    idx = np.random.permutation(T)[:I]
    idx2 = np.random.permutation(Z)[:I]
    fd = mx_kscale(D)
    fi = mx_kscale(I)
    ti = np.ones(T)
    ti[idx] = fi
    keysp = pack_weight(n((D, T)) / fd[:, None], "e2m1")
    return {
        "query": (n((D, Q)) * 1.0 / np.sqrt(D) * fd[:, None]).astype(np.float32),
        "query2": (n((D, Q)) * 1.0 / np.sqrt(D) * fd[:, None]).astype(np.float32),
        "keys_words": keysp[0],
        "keys_scales": keysp[1],
        "pages": (n((D, Z)) / fd[:, None]).astype(np.float32),
        "os": (np.random.uniform(0.02, 0.08, (1, I)) * fi).astype(np.float32),
        "vals": (n((E, T)) / ti).astype(np.float32),
        "offs": striped(idx),
        "offs2": striped(idx2),
    }


def reference(query, query2, keys_words, keys_scales, pages, os, vals, offs, offs2):
    idx = unstriped(offs)
    idx2 = unstriped(offs2)
    keysu = unpack_weight(keys_words, keys_scales, "e2m1")
    queryq = mxq(f64(query), 0, "e4m3")
    keysidxg = keysu[:, idx]
    a = queryq.T @ keysidxg
    query2q = mxq(f64(query2), 0, "e4m3")
    pagesq = mxq(f64(pages), 0, "e4m3")
    h0 = query2q.T @ pagesq
    s = np.maximum(a, h0[:, idx2])
    w = np.maximum(s, 0.0)
    wo1 = w * f64(os)
    wt1 = wo1.T
    vt1 = f64(vals)[:, idx].T
    vt1q = mxq(vt1, 0, "e4m3")
    wt1q = mxq(wt1, 0, "e4m3")
    o = vt1q.T @ wt1q
    words, scales = planes(o)
    return o, words, scales

@@ -1,0 +1,235 @@
+from contextlib import ExitStack
+
+import concourse.mybir as mybir
+from concourse.masks import make_identity
+
+D, T, I, Q, E, Z = 512, 2048, 512, 256, 512, 1024
+FLOPS = 2 * D * Q * I + 2 * D * Q * Z + 2 * I * E * Q
+
+F32 = mybir.dt.float32
+BF16 = mybir.dt.bfloat16
+I32 = mybir.dt.int32
+U32 = mybir.dt.uint32
+U16 = mybir.dt.uint16
+U8 = mybir.dt.uint8
+E4M3X4 = mybir.dt.float8_e4m3fn_x4
+E2M1X4 = mybir.dt.float4_e2m1fn_x4
+ALU = mybir.AluOpType
+COPY = mybir.ActivationFunctionType.Copy
+
+P = 128
+PACK = 4
+BANK = 512
+RUN = 4
+PAGE_SPLIT = 320
+LAST_SPLIT = 20
+
+
+def weave(copy, woven, rows):
+    copy(
+        out=woven.rearrange("p (c i) t -> p c t i", i=RUN),
+        in_=rows.rearrange("p t (c i) -> p c t i", i=RUN),
+    )
+
+
+def quantize(nc, codes, scales, woven):
+    nc.vector.quantize_mx(out=codes.bitcast(E4M3X4), scales=scales, in_=woven.rearrange("p c t -> p (c t)"))
+
+
+def tile_attend_widelarger_read_lean_pl_kernel(
+    tc, query, query2, keys_words, keys_scales, pages, slot_factor, vals, offs, offs2, out_0, out_1, out_2
+):
+    nc = tc.nc
+    with ExitStack() as ctx:
+        sb = ctx.enter_context(tc.tile_pool(name="sb", bufs=1))
+        ps = ctx.enter_context(tc.psum_pool(name="ps", bufs=1))
+
+        def mx_operand(name, width, tag):
+            woven = sb.tile([P, width, PACK], BF16, name=name + "_woven", tag=tag, align_bytes=64)
+            codes = sb.tile([P, width], U32, name=name + "_codes", align_bytes=64)
+            scales = sb.tile([P, width], U8, name=name + "_scales", align_bytes=64)
+            return woven, codes, scales
+
+        tokens = sb.tile([P, I // 16], U16, name="tokens")
+        page_list = sb.tile([P, I // 16], U16, name="page_list")
+        key_words = sb.tile([P, T], U16, name="key_words", align_bytes=64)
+        key_bytes = sb.tile([P, T], U8, name="key_bytes", align_bytes=64)
+        q_rows = sb.tile([P, PACK, Q], F32, name="q_rows")
+        q2_rows = sb.tile([P, PACK, Q], F32, name="q2_rows")
+        page_rows = [sb.tile([P, PACK, BANK], F32, name="page_rows%d" % h) for h in range(2)]
+        val_rows = [sb.tile([P, T], F32, name="val_rows%d" % j, tag="val_rows%d" % j, align_bytes=64) for j in range(PACK)]
+        factor = sb.tile([P, PACK], F32, name="factor")
+        ident = sb.tile([P, P], F32, name="ident")
+
+        nc.vector.memset(key_bytes[:].bitcast(I32), 0)
+        make_identity(nc, ident[:])
+
+        pages_v = pages.rearrange("(p t) z -> p t z", t=PACK)
+        vals_v = vals.rearrange("(p j) c -> p j c", j=PACK)
+        nc.sync.dma_start(out=key_words[:].bitcast(I32), in_=keys_words[0].bitcast(I32))
+        nc.sync.dma_start(tokens[:], offs)
+        for quad in range(4):
+            nc.sync.dma_start(
+                out=key_bytes[32 * quad : 32 * quad + 4, :].bitcast(I32),
+                in_=keys_scales[0][4 * quad : 4 * quad + 4, :].bitcast(I32),
+            )
+        nc.sync.dma_start(out=q2_rows[:], in_=query2.rearrange("(p t) q -> p t q", t=PACK))
+        for h in range(2):
+            nc.sync.dma_start(out=page_rows[h][:], in_=pages_v[:, :, h * BANK : (h + 1) * BANK])
+        nc.sync.dma_start(out=q_rows[:], in_=query.rearrange("(p t) q -> p t q", t=PACK))
+        nc.sync.dma_start(page_list[:], offs2)
+        nc.sync.dma_start(out=factor[:], in_=slot_factor[0].rearrange("(p t) -> p t", t=PACK))
+        for j in range(PACK):
+            nc.sync.dma_start(out=val_rows[j][:], in_=vals_v[:, j, :])
+
+        listed_words = sb.tile([P, I], U16, name="listed_words", align_bytes=64)
+        listed_bytes = sb.tile([P, I], U8, name="listed_bytes", align_bytes=64)
+        nc.vector.tensor_copy(listed_words[:], key_words[:].indirect(tokens[:]))
+        nc.vector.tensor_copy(listed_bytes[:], key_bytes[:].indirect(tokens[:]))
+
+        q2_woven, q2_codes, q2_scales = mx_operand("q2", Q, "q2_woven")
+        weave(nc.scalar.copy, q2_woven[:], q2_rows[:])
+        quantize(nc, q2_codes[:], q2_scales[:], q2_woven[:])
+
+        h0 = [sb.tile([P, Z], F32, name="h0_%d" % g, tag="h0_%d" % g, align_bytes=64) for g in range(2)]
+        for h, pieces in enumerate(([(0, BANK, 0)], [(0, BANK // 2, 2), (BANK // 2, BANK, 0)])):
+            woven, codes, scales = mx_operand("page%d" % h, BANK, "page_woven%d" % h)
+            for lo, hi, first_bank in pieces:
+                weave(nc.vector.tensor_copy, woven[:, lo:hi, :], page_rows[h][:, :, lo:hi])
+            for lo, hi, first_bank in pieces:
+                quantize(nc, codes[:, lo:hi], scales[:, lo:hi], woven[:, lo:hi, :])
+                for g in range(2):
+                    cols = slice(g * P, (g + 1) * P)
+                    bank = ps.tile([P, hi - lo], F32, name="h0_bank", tag="bank%d" % (first_bank + g))
+                    nc.tensor.matmul_mx(
+                        out=bank[:],
+                        lhsT=q2_codes[:, cols].bitcast(E4M3X4),
+                        lhsT_scale=q2_scales[:, cols],
+                        rhs=codes[:, lo:hi].bitcast(E4M3X4),
+                        rhs_scale=scales[:, lo:hi],
+                        start=True,
+                        stop=True,
+                    )
+                    nc.scalar.copy(out=h0[g][:, h * BANK + lo : h * BANK + hi], in_=bank[:])
+
+        q_woven, q_codes, q_scales = mx_operand("q", Q, "page_woven1")
+        weave(nc.vector.tensor_copy, q_woven[:], q_rows[:])
+        quantize(nc, q_codes[:], q_scales[:], q_woven[:])
+        a_banks = []
+        for g in range(2):
+            cols = slice(g * P, (g + 1) * P)
+            a_bank = ps.tile([P, I], F32, name="a_bank", tag="bank%d" % (4 + g))
+            nc.tensor.matmul_mx(
+                out=a_bank[:],
+                lhsT=q_codes[:, cols].bitcast(E4M3X4),
+                lhsT_scale=q_scales[:, cols],
+                rhs=listed_words[:].bitcast(E2M1X4),
+                rhs_scale=listed_bytes[:],
+                start=True,
+                stop=True,
+            )
+            a_banks.append(a_bank)
+
+        w_woven, w_codes, w_scales = mx_operand("w", Q, "w_woven")
+        looked = [sb.tile([P, I], F32, name="looked%d" % g, tag="looked%d" % g, align_bytes=64) for g in range(2)]
+        dealt = [sb.tile([P, PACK, P], F32, name="dealt%d" % g) for g in range(2)]
+        nc.vector.tensor_copy(looked[0][:], h0[0][:].indirect(page_list[:]))
+        nc.scalar.activation(looked[1][:], h0[1][:].indirect(page_list[:]), COPY)
+        turned = []
+        for g in range(2):
+            nc.vector.scalar_tensor_tensor(
+                out=dealt[g][:].rearrange("q t m -> q m t"),
+                in0=a_banks[g][:].rearrange("q (m t) -> q m t", t=PACK),
+                scalar=0.0,
+                in1=looked[g][:].rearrange("q (m t) -> q m t", t=PACK),
+                op0=ALU.max,
+                op1=ALU.max,
+            )
+            w_bank = ps.tile([P, PACK, P], F32, name="w_bank", tag="bank%d" % g)
+            for t in range(PACK):
+                nc.tensor.transpose(w_bank[:, t, :], dealt[g][:, t, :], ident[:])
+            turned.append(w_bank)
+        for g in range(2):
+            nc.vector.tensor_tensor(
+                out=w_woven[:, g * P : (g + 1) * P, :],
+                in0=turned[g][:].rearrange("p t q -> p q t"),
+                in1=factor[:].unsqueeze(1).to_broadcast([P, P, PACK]),
+                op=ALU.mult,
+            )
+        quantize(nc, w_codes[:], w_scales[:], w_woven[:])
+
+        out_v = out_0.rearrange("(p j) q -> p j q", j=PACK)
+        o_woven, o_codes, o_scales = mx_operand("o", Q, "o_woven")
+        v_woven, v_codes, v_scales = {}, {}, {}
+        last = PACK - 1
+
+        def pick_values(j):
+            picked = sb.tile([P, I], BF16, name="picked%d" % j, tag="h0_1" if j == 0 else "val_rows0", align_bytes=64)
+            if j < last:
+                nc.scalar.activation(picked[:], val_rows[j][:].indirect(tokens[:]), COPY)
+            else:
+                n = 16 * LAST_SPLIT
+                nc.vector.tensor_copy(picked[:, :n], val_rows[j][:].indirect(tokens[:, :LAST_SPLIT]))
+                nc.scalar.activation(picked[:, n:], val_rows[j][:].indirect(tokens[:, LAST_SPLIT:]), COPY)
+            return picked
+
+        def turn_picked(j, picked, bank):
+            pairs = picked[:].bitcast(F32)
+            v_bank = ps.tile([P, 2, P], F32, name="v_bank", tag="bank%d" % bank)
+            for u in range(2):
+                nc.tensor.transpose(v_bank[:, u, :], pairs[:, u::2], ident[:])
+            v_woven[j] = sb.tile([P, P, PACK], BF16, name="v_woven%d" % j, tag="val_rows1" if j == 0 else "v_woven%d" % j, align_bytes=64)
+            nc.scalar.copy(out=v_woven[j][:].bitcast(F32), in_=v_bank[:].rearrange("p u m -> p m u"))
+
+        def quantize_values(j, tag):
+            v_codes[j] = sb.tile([P, P], U32, name="v_codes%d" % j, tag=tag, align_bytes=64)
+            v_scales[j] = sb.tile([P, P], U8, name="v_scales%d" % j, align_bytes=64)
+            quantize(nc, v_codes[j][:], v_scales[j][:], v_woven[j][:])
+
+        def multiply(j):
+            for g in range(2):
+                cols = slice(g * P, (g + 1) * P)
+                nc.tensor.matmul_mx(
+                    out=o_banks[g][:, j, :],
+                    lhsT=v_codes[j][:].bitcast(E4M3X4),
+                    lhsT_scale=v_scales[j][:],
+                    rhs=w_codes[:, cols].bitcast(E4M3X4),
+                    rhs_scale=w_scales[:, cols],
+                    start=True,
+                    stop=True,
+                )
+
+        def store_rows(j, copy, queue, tag):
+            result = sb.tile([P, Q], F32, name="result%d" % j, tag=tag, align_bytes=64)
+            for g in (1, 0):
+                copy(out=result[:, g * P : (g + 1) * P], in_=o_banks[g][:, j, :])
+            queue.dma_start(out=out_v[:, j, :], in_=result[:])
+
+        picked0 = pick_values(0)
+        picked1 = pick_values(1)
+        turn_picked(0, picked0, 6)
+        quantize_values(0, "looked1")
+        turn_picked(1, picked1, 2)
+        quantize_values(1, "w_woven")
+        o_banks = [ps.tile([P, PACK, P], F32, name="o_bank%d" % g, tag="bank%d" % (2 + g)) for g in range(2)]
+        for j in range(2):
+            multiply(j)
+            store_rows(j, nc.vector.tensor_copy, nc.sync, "result%d" % j)
+        turn_picked(2, pick_values(2), 6)
+        turn_picked(3, pick_values(3), 7)
+        quantize_values(2, "val_rows3")
+        multiply(2)
+        quantize_values(3, "v_codes3")
+        store_rows(2, nc.scalar.copy, nc.sync, "val_rows3")
+        multiply(3)
+        nc.vector.tensor_copy(out=o_woven[:, :P, :], in_=o_banks[0][:].rearrange("p j q -> p q j"))
+        nc.scalar.copy(out=o_woven[:, P:, :], in_=o_banks[1][:].rearrange("p j q -> p q j"))
+        quantize(nc, o_codes[:], o_scales[:], o_woven[:])
+        store_rows(3, nc.scalar.copy, nc.scalar, "result3")
+        nc.sync.dma_start(out=out_1[0].rearrange("p c r -> p (c r)").bitcast(I32), in_=o_codes[:].bitcast(I32))
+        for quad in range(4):
+            queue = nc.sync if quad < 2 else nc.scalar
+            queue.dma_start(
+                out=out_2[0][4 * quad : 4 * quad + 4, :].bitcast(I32),
+                in_=o_scales[32 * quad : 32 * quad + 4, :].bitcast(I32),
+            )

@@ -19,10 +19,12 @@ COPY = mybir.ActivationFunctionType.Copy
 
 P = 128
 PACK = 4
-BANK = 512
+GROUPS = Q // P
+QUADS = 4
+HALF = Z // 2
 RUN = 4
-PAGE_SPLIT = 320
-LAST_SPLIT = 20
+PER_COLUMN = 16
+VECTOR_SHARE = 18
 
 
 def weave(copy, woven, rows):
@@ -36,6 +38,22 @@ def quantize(nc, codes, scales, woven):
     nc.vector.quantize_mx(out=codes.bitcast(E4M3X4), scales=scales, in_=woven.rearrange("p c t -> p (c t)"))
 
 
+def product(nc, out, codes, scales, moving, moving_scales):
+    nc.tensor.matmul_mx(
+        out=out, lhsT=codes.bitcast(E4M3X4), lhsT_scale=scales, rhs=moving, rhs_scale=moving_scales, start=True, stop=True
+    )
+
+
+def turn_pairs(nc, bank, slots, ident):
+    pairs = slots.bitcast(F32)
+    for u in range(2):
+        nc.tensor.transpose(bank[:, u, :], pairs[:, u::2], ident)
+
+
+def weave_pairs(copy, woven, bank):
+    copy(out=woven.bitcast(F32), in_=bank.rearrange("p u c -> p c u"))
+
+
 def tile_attend_widelarger_read_lean_pl_kernel(
     tc, query, query2, keys_words, keys_scales, pages, slot_factor, vals, offs, offs2, out_0, out_1, out_2
 ):
@@ -44,191 +62,184 @@ def tile_attend_widelarger_read_lean_pl_kernel(
         sb = ctx.enter_context(tc.tile_pool(name="sb", bufs=1))
         ps = ctx.enter_context(tc.psum_pool(name="ps", bufs=1))
 
-        def mx_operand(name, width, tag):
-            woven = sb.tile([P, width, PACK], BF16, name=name + "_woven", tag=tag, align_bytes=64)
-            codes = sb.tile([P, width], U32, name=name + "_codes", align_bytes=64)
-            scales = sb.tile([P, width], U8, name=name + "_scales", align_bytes=64)
-            return woven, codes, scales
+        def tile(name, shape, dtype, tag=None):
+            return sb.tile(shape, dtype, name=name, tag=tag or name, align_bytes=64)
 
-        tokens = sb.tile([P, I // 16], U16, name="tokens")
-        page_list = sb.tile([P, I // 16], U16, name="page_list")
-        key_words = sb.tile([P, T], U16, name="key_words", align_bytes=64)
-        key_bytes = sb.tile([P, T], U8, name="key_bytes", align_bytes=64)
-        q_rows = sb.tile([P, PACK, Q], F32, name="q_rows")
-        q2_rows = sb.tile([P, PACK, Q], F32, name="q2_rows")
-        page_rows = [sb.tile([P, PACK, BANK], F32, name="page_rows%d" % h) for h in range(2)]
-        val_rows = [sb.tile([P, T], F32, name="val_rows%d" % j, tag="val_rows%d" % j, align_bytes=64) for j in range(PACK)]
-        factor = sb.tile([P, PACK], F32, name="factor")
-        ident = sb.tile([P, P], F32, name="ident")
+        def bank(number, shape):
+            return ps.tile(shape, F32, name="bank%d" % number, tag="bank%d" % number)
 
-        nc.vector.memset(key_bytes[:].bitcast(I32), 0)
+        def quantized(name, woven, tag=None):
+            width = woven.shape[1]
+            codes = tile(name + "_codes", [P, width], U32, tag)
+            scales = tile(name + "_scales", [P, width], U8)
+            quantize(nc, codes[:], scales[:], woven[:])
+            return codes, scales
+
+        def group(g):
+            return slice(g * P, (g + 1) * P)
+
+        tokens = sb.tile([P, I // PER_COLUMN], U16, name="tokens")
+        page_list = sb.tile([P, I // PER_COLUMN], U16, name="page_list")
+        key_words = tile("key_words", [P, T], U16)
+        key_bytes = tile("key_bytes", [P, T], U8)
+        q_rows = tile("q_rows", [P, PACK, Q], F32)
+        q2_rows = tile("q2_rows", [P, PACK, Q], F32)
+        page_rows = [tile("page_rows%d" % h, [P, PACK, HALF], F32) for h in range(2)]
+        val_rows = [tile("val_rows%d" % j, [P, T], F32) for j in range(PACK)]
+        factor = tile("factor", [P, PACK], F32)
+        ident = tile("ident", [P, P], F32)
+
+        nc.gpsimd.memset(key_bytes[:].bitcast(I32), 0)
         make_identity(nc, ident[:])
 
-        pages_v = pages.rearrange("(p t) z -> p t z", t=PACK)
-        vals_v = vals.rearrange("(p j) c -> p j c", j=PACK)
-        nc.sync.dma_start(out=key_words[:].bitcast(I32), in_=keys_words[0].bitcast(I32))
+        pages_by_place = pages.rearrange("(p t) z -> p t z", t=PACK)
+        vals_by_plane = vals.rearrange("(p j) c -> p j c", j=PACK)
+        nc.sync.dma_start(out=page_rows[0][:], in_=pages_by_place[:, :, :HALF])
         nc.sync.dma_start(tokens[:], offs)
-        for quad in range(4):
+        nc.sync.dma_start(out=factor[:], in_=slot_factor[0].rearrange("(p t) -> p t", t=PACK))
+        for quad in range(QUADS):
             nc.sync.dma_start(
                 out=key_bytes[32 * quad : 32 * quad + 4, :].bitcast(I32),
                 in_=keys_scales[0][4 * quad : 4 * quad + 4, :].bitcast(I32),
             )
         nc.sync.dma_start(out=q2_rows[:], in_=query2.rearrange("(p t) q -> p t q", t=PACK))
-        for h in range(2):
-            nc.sync.dma_start(out=page_rows[h][:], in_=pages_v[:, :, h * BANK : (h + 1) * BANK])
+        nc.sync.dma_start(out=key_words[:].bitcast(I32), in_=keys_words[0].bitcast(I32))
+        nc.sync.dma_start(out=page_rows[1][:], in_=pages_by_place[:, :, HALF:])
         nc.sync.dma_start(out=q_rows[:], in_=query.rearrange("(p t) q -> p t q", t=PACK))
         nc.sync.dma_start(page_list[:], offs2)
-        nc.sync.dma_start(out=factor[:], in_=slot_factor[0].rearrange("(p t) -> p t", t=PACK))
         for j in range(PACK):
-            nc.sync.dma_start(out=val_rows[j][:], in_=vals_v[:, j, :])
+            nc.sync.dma_start(out=val_rows[j][:], in_=vals_by_plane[:, j, :])
 
-        listed_words = sb.tile([P, I], U16, name="listed_words", align_bytes=64)
-        listed_bytes = sb.tile([P, I], U8, name="listed_bytes", align_bytes=64)
-        nc.vector.tensor_copy(listed_words[:], key_words[:].indirect(tokens[:]))
+        h0 = [tile("h0_%d" % g, [P, Z], F32) for g in range(GROUPS)]
+
+        def quantize_pages(name, rows):
+            woven = tile(name + "_woven", [P, rows.shape[2], PACK], BF16)
+            weave(nc.vector.tensor_copy, woven[:], rows)
+            return quantized(name, woven)
+
+        def score_pages(operand, first_page, first_bank):
+            codes, scales = operand
+            width = codes.shape[1]
+            for g in range(GROUPS):
+                h0_bank = bank(first_bank + g, [P, width])
+                product(nc, h0_bank[:], q2_codes[:, group(g)], q2_scales[:, group(g)], codes[:].bitcast(E4M3X4), scales[:])
+                nc.scalar.copy(out=h0[g][:, first_page : first_page + width], in_=h0_bank[:])
+
+        first_half = quantize_pages("pages0", page_rows[0][:])
+        listed_bytes = tile("listed_bytes", [P, I], U8)
         nc.vector.tensor_copy(listed_bytes[:], key_bytes[:].indirect(tokens[:]))
-
-        q2_woven, q2_codes, q2_scales = mx_operand("q2", Q, "q2_woven")
+        q2_woven = tile("q2_woven", [P, Q, PACK], BF16)
         weave(nc.scalar.copy, q2_woven[:], q2_rows[:])
-        quantize(nc, q2_codes[:], q2_scales[:], q2_woven[:])
+        q2_codes, q2_scales = quantized("q2", q2_woven)
+        score_pages(first_half, 0, 0)
+        listed_words = tile("listed_words", [P, I], U16, "q2_woven")
+        nc.vector.tensor_copy(listed_words[:], key_words[:].indirect(tokens[:]))
+        quarter = HALF // 2
+        score_pages(quantize_pages("pages1", page_rows[1][:, :, :quarter]), HALF, 2)
+        score_pages(quantize_pages("pages2", page_rows[1][:, :, quarter:]), HALF + quarter, 0)
 
-        h0 = [sb.tile([P, Z], F32, name="h0_%d" % g, tag="h0_%d" % g, align_bytes=64) for g in range(2)]
-        for h, pieces in enumerate(([(0, BANK, 0)], [(0, BANK // 2, 2), (BANK // 2, BANK, 0)])):
-            woven, codes, scales = mx_operand("page%d" % h, BANK, "page_woven%d" % h)
-            for lo, hi, first_bank in pieces:
-                weave(nc.vector.tensor_copy, woven[:, lo:hi, :], page_rows[h][:, :, lo:hi])
-            for lo, hi, first_bank in pieces:
-                quantize(nc, codes[:, lo:hi], scales[:, lo:hi], woven[:, lo:hi, :])
-                for g in range(2):
-                    cols = slice(g * P, (g + 1) * P)
-                    bank = ps.tile([P, hi - lo], F32, name="h0_bank", tag="bank%d" % (first_bank + g))
-                    nc.tensor.matmul_mx(
-                        out=bank[:],
-                        lhsT=q2_codes[:, cols].bitcast(E4M3X4),
-                        lhsT_scale=q2_scales[:, cols],
-                        rhs=codes[:, lo:hi].bitcast(E4M3X4),
-                        rhs_scale=scales[:, lo:hi],
-                        start=True,
-                        stop=True,
-                    )
-                    nc.scalar.copy(out=h0[g][:, h * BANK + lo : h * BANK + hi], in_=bank[:])
-
-        q_woven, q_codes, q_scales = mx_operand("q", Q, "page_woven1")
+        q_woven = tile("q_woven", [P, Q, PACK], BF16, "pages2_woven")
         weave(nc.vector.tensor_copy, q_woven[:], q_rows[:])
-        quantize(nc, q_codes[:], q_scales[:], q_woven[:])
-        a_banks = []
-        for g in range(2):
-            cols = slice(g * P, (g + 1) * P)
-            a_bank = ps.tile([P, I], F32, name="a_bank", tag="bank%d" % (4 + g))
-            nc.tensor.matmul_mx(
-                out=a_bank[:],
-                lhsT=q_codes[:, cols].bitcast(E4M3X4),
-                lhsT_scale=q_scales[:, cols],
-                rhs=listed_words[:].bitcast(E2M1X4),
-                rhs_scale=listed_bytes[:],
-                start=True,
-                stop=True,
+        q_codes, q_scales = quantized("q", q_woven)
+        a_banks = [bank(4 + g, [P, I]) for g in range(GROUPS)]
+        for g in range(GROUPS):
+            product(
+                nc, a_banks[g][:], q_codes[:, group(g)], q_scales[:, group(g)], listed_words[:].bitcast(E2M1X4), listed_bytes[:]
             )
-            a_banks.append(a_bank)
 
-        w_woven, w_codes, w_scales = mx_operand("w", Q, "w_woven")
-        looked = [sb.tile([P, I], F32, name="looked%d" % g, tag="looked%d" % g, align_bytes=64) for g in range(2)]
-        dealt = [sb.tile([P, PACK, P], F32, name="dealt%d" % g) for g in range(2)]
+        factor_bank = bank(7, [P, PACK, P])
+        for t in range(PACK):
+            nc.tensor.transpose(factor_bank[:, t, :], factor[:, t : t + 1].to_broadcast([P, P]), ident[:])
+
+        looked = [tile("looked%d" % g, [P, I], F32) for g in range(GROUPS)]
+        middle = I // 2
         nc.vector.tensor_copy(looked[0][:], h0[0][:].indirect(page_list[:]))
-        nc.scalar.activation(looked[1][:], h0[1][:].indirect(page_list[:]), COPY)
-        turned = []
-        for g in range(2):
-            nc.vector.scalar_tensor_tensor(
-                out=dealt[g][:].rearrange("q t m -> q m t"),
-                in0=a_banks[g][:].rearrange("q (m t) -> q m t", t=PACK),
-                scalar=0.0,
-                in1=looked[g][:].rearrange("q (m t) -> q m t", t=PACK),
-                op0=ALU.max,
-                op1=ALU.max,
-            )
-            w_bank = ps.tile([P, PACK, P], F32, name="w_bank", tag="bank%d" % g)
-            for t in range(PACK):
-                nc.tensor.transpose(w_bank[:, t, :], dealt[g][:, t, :], ident[:])
-            turned.append(w_bank)
-        for g in range(2):
-            nc.vector.tensor_tensor(
-                out=w_woven[:, g * P : (g + 1) * P, :],
-                in0=turned[g][:].rearrange("p t q -> p q t"),
-                in1=factor[:].unsqueeze(1).to_broadcast([P, P, PACK]),
-                op=ALU.mult,
-            )
-        quantize(nc, w_codes[:], w_scales[:], w_woven[:])
+        nc.scalar.activation(looked[1][:, middle:], h0[1][:].indirect(page_list[:, middle // PER_COLUMN :]), COPY)
+        nc.vector.tensor_copy(looked[1][:, :middle], h0[1][:].indirect(page_list[:, : middle // PER_COLUMN]))
 
-        out_v = out_0.rearrange("(p j) q -> p j q", j=PACK)
-        o_woven, o_codes, o_scales = mx_operand("o", Q, "o_woven")
-        v_woven, v_codes, v_scales = {}, {}, {}
-        last = PACK - 1
-
-        def pick_values(j):
-            picked = sb.tile([P, I], BF16, name="picked%d" % j, tag="h0_1" if j == 0 else "val_rows0", align_bytes=64)
-            if j < last:
-                nc.scalar.activation(picked[:], val_rows[j][:].indirect(tokens[:]), COPY)
-            else:
-                n = 16 * LAST_SPLIT
-                nc.vector.tensor_copy(picked[:, :n], val_rows[j][:].indirect(tokens[:, :LAST_SPLIT]))
-                nc.scalar.activation(picked[:, n:], val_rows[j][:].indirect(tokens[:, LAST_SPLIT:]), COPY)
+        def pick_values(j, tag=None):
+            picked = tile("picked%d" % j, [P, I], BF16, tag)
+            nc.scalar.activation(picked[:], val_rows[j][:].indirect(tokens[:]), COPY)
             return picked
 
-        def turn_picked(j, picked, bank):
-            pairs = picked[:].bitcast(F32)
-            v_bank = ps.tile([P, 2, P], F32, name="v_bank", tag="bank%d" % bank)
-            for u in range(2):
-                nc.tensor.transpose(v_bank[:, u, :], pairs[:, u::2], ident[:])
-            v_woven[j] = sb.tile([P, P, PACK], BF16, name="v_woven%d" % j, tag="val_rows1" if j == 0 else "v_woven%d" % j, align_bytes=64)
-            nc.scalar.copy(out=v_woven[j][:].bitcast(F32), in_=v_bank[:].rearrange("p u m -> p m u"))
+        def turn_values(picked, number):
+            v_bank = bank(number, [P, 2, P])
+            turn_pairs(nc, v_bank[:], picked[:], ident[:])
+            return v_bank
 
-        def quantize_values(j, tag):
-            v_codes[j] = sb.tile([P, P], U32, name="v_codes%d" % j, tag=tag, align_bytes=64)
-            v_scales[j] = sb.tile([P, P], U8, name="v_scales%d" % j, align_bytes=64)
-            quantize(nc, v_codes[j][:], v_scales[j][:], v_woven[j][:])
+        def weave_values(j, v_bank, tag=None):
+            woven = tile("v_woven%d" % j, [P, P, PACK], BF16, tag)
+            weave_pairs(nc.scalar.copy, woven[:], v_bank[:])
+            return woven
+
+        v_bank0 = turn_values(pick_values(0), 6)
+
+        scores = [tile("scores%d" % g, [P, I], F32) for g in range(GROUPS)]
+        for g in range(GROUPS):
+            nc.vector.scalar_tensor_tensor(
+                out=scores[g][:], in0=a_banks[g][:], scalar=0.0, in1=looked[g][:], op0=ALU.max, op1=ALU.max
+            )
+        weights = [tile("weights0", [P, I], BF16, "picked0"), tile("weights1", [P, I], BF16)]
+        w_banks = [bank(g, [P, 2, P]) for g in range(GROUPS)]
+        for g in range(GROUPS):
+            nc.vector.tensor_tensor(
+                out=weights[g][:].rearrange("q (m t) -> q m t", t=PACK),
+                in0=scores[g][:].rearrange("q (m t) -> q m t", t=PACK),
+                in1=factor_bank[:].rearrange("q t m -> q m t"),
+                op=ALU.mult,
+            )
+            turn_pairs(nc, w_banks[g][:], weights[g][:], ident[:])
+        w_woven = tile("w_woven", [P, Q, PACK], BF16)
+        for g in range(GROUPS):
+            weave_pairs(nc.vector.tensor_copy, w_woven[:, group(g), :], w_banks[g][:])
+        w_codes, w_scales = quantized("w", w_woven)
+
+        picked1 = pick_values(1, "val_rows0")
+        picked2 = pick_values(2)
+        v_operands = [quantized("v0", weave_values(0, v_bank0, "val_rows1"), "w_woven")]
+        v_operands.append(quantized("v1", weave_values(1, turn_values(picked1, 2), "val_rows2")))
+        v_woven2 = weave_values(2, turn_values(picked2, 6))
+
+        out_by_plane = out_0.rearrange("(p j) q -> p j q", j=PACK)
+        o_banks = [bank(6, [P, PACK, P]), bank(3, [P, PACK, P])]
 
         def multiply(j):
-            for g in range(2):
-                cols = slice(g * P, (g + 1) * P)
-                nc.tensor.matmul_mx(
-                    out=o_banks[g][:, j, :],
-                    lhsT=v_codes[j][:].bitcast(E4M3X4),
-                    lhsT_scale=v_scales[j][:],
-                    rhs=w_codes[:, cols].bitcast(E4M3X4),
-                    rhs_scale=w_scales[:, cols],
-                    start=True,
-                    stop=True,
+            codes, scales = v_operands[j]
+            for g in range(GROUPS):
+                product(
+                    nc, o_banks[g][:, j, :], codes[:], scales[:], w_codes[:, group(g)].bitcast(E4M3X4), w_scales[:, group(g)]
                 )
 
-        def store_rows(j, copy, queue, tag):
-            result = sb.tile([P, Q], F32, name="result%d" % j, tag=tag, align_bytes=64)
-            for g in (1, 0):
-                copy(out=result[:, g * P : (g + 1) * P], in_=o_banks[g][:, j, :])
-            queue.dma_start(out=out_v[:, j, :], in_=result[:])
+        def store_planes(first, end, copy, queue, tag=None):
+            result = tile("result%d" % first, [P, end - first, Q], F32, tag)
+            for g in reversed(range(GROUPS)):
+                copy(out=result[:, :, group(g)], in_=o_banks[g][:, first:end, :])
+            queue.dma_start(out=out_by_plane[:, first:end, :], in_=result[:])
 
-        picked0 = pick_values(0)
-        picked1 = pick_values(1)
-        turn_picked(0, picked0, 6)
-        quantize_values(0, "looked1")
-        turn_picked(1, picked1, 2)
-        quantize_values(1, "w_woven")
-        o_banks = [ps.tile([P, PACK, P], F32, name="o_bank%d" % g, tag="bank%d" % (2 + g)) for g in range(2)]
-        for j in range(2):
-            multiply(j)
-            store_rows(j, nc.vector.tensor_copy, nc.sync, "result%d" % j)
-        turn_picked(2, pick_values(2), 6)
-        turn_picked(3, pick_values(3), 7)
-        quantize_values(2, "val_rows3")
+        multiply(0)
+        multiply(1)
+
+        last = PACK - 1
+        picked3 = tile("picked3", [P, I], BF16)
+        share = VECTOR_SHARE * PER_COLUMN
+        nc.vector.tensor_copy(picked3[:, :share], val_rows[last][:].indirect(tokens[:, :VECTOR_SHARE]))
+        nc.scalar.activation(picked3[:, share:], val_rows[last][:].indirect(tokens[:, VECTOR_SHARE:]), COPY)
+        v_woven3 = weave_values(last, turn_values(picked3, 7))
+        v_operands.append(quantized("v2", v_woven2, "val_rows3"))
+        store_planes(0, 2, nc.vector.tensor_copy, nc.sync, "v_woven2")
         multiply(2)
-        quantize_values(3, "v_codes3")
-        store_rows(2, nc.scalar.copy, nc.sync, "val_rows3")
-        multiply(3)
-        nc.vector.tensor_copy(out=o_woven[:, :P, :], in_=o_banks[0][:].rearrange("p j q -> p q j"))
-        nc.scalar.copy(out=o_woven[:, P:, :], in_=o_banks[1][:].rearrange("p j q -> p q j"))
-        quantize(nc, o_codes[:], o_scales[:], o_woven[:])
-        store_rows(3, nc.scalar.copy, nc.scalar, "result3")
+        v_operands.append(quantized("v3", v_woven3))
+        store_planes(2, last, nc.scalar.copy, nc.sync)
+        multiply(last)
+
+        o_woven = tile("o_woven", [P, Q, PACK], BF16)
+        for g, copy in enumerate((nc.vector.tensor_copy, nc.scalar.copy)):
+            copy(out=o_woven[:, group(g), :], in_=o_banks[g][:].rearrange("p j q -> p q j"))
+        o_codes, o_scales = quantized("o", o_woven)
+        store_planes(last, PACK, nc.scalar.copy, nc.scalar)
         nc.sync.dma_start(out=out_1[0].rearrange("p c r -> p (c r)").bitcast(I32), in_=o_codes[:].bitcast(I32))
-        for quad in range(4):
-            queue = nc.sync if quad < 2 else nc.scalar
+        for quad in range(QUADS):
+            queue = nc.sync if quad < QUADS // 2 else nc.scalar
             queue.dma_start(
                 out=out_2[0][4 * quad : 4 * quad + 4, :].bitcast(I32),
                 in_=o_scales[32 * quad : 32 * quad + 4, :].bitcast(I32),

@@ -24,7 +24,8 @@ QUADS = 4
 HALF = Z // 2
 RUN = 4
 PER_COLUMN = 16
-VECTOR_SHARE = 18
+VECTOR_SHARE = 20
+OUT_SHARE = 160
 
 
 def weave(copy, woven, rows):
@@ -94,7 +95,7 @@ def tile_attend_widelarger_read_lean_pl_kernel(
 
         pages_by_place = pages.rearrange("(p t) z -> p t z", t=PACK)
         vals_by_plane = vals.rearrange("(p j) c -> p j c", j=PACK)
-        nc.sync.dma_start(out=page_rows[0][:], in_=pages_by_place[:, :, :HALF])
+        nc.sync.dma_start(out=q2_rows[:], in_=query2.rearrange("(p t) q -> p t q", t=PACK))
         nc.sync.dma_start(tokens[:], offs)
         nc.sync.dma_start(out=factor[:], in_=slot_factor[0].rearrange("(p t) -> p t", t=PACK))
         for quad in range(QUADS):
@@ -102,10 +103,10 @@ def tile_attend_widelarger_read_lean_pl_kernel(
                 out=key_bytes[32 * quad : 32 * quad + 4, :].bitcast(I32),
                 in_=keys_scales[0][4 * quad : 4 * quad + 4, :].bitcast(I32),
             )
-        nc.sync.dma_start(out=q2_rows[:], in_=query2.rearrange("(p t) q -> p t q", t=PACK))
-        nc.sync.dma_start(out=key_words[:].bitcast(I32), in_=keys_words[0].bitcast(I32))
-        nc.sync.dma_start(out=page_rows[1][:], in_=pages_by_place[:, :, HALF:])
+        for h in range(2):
+            nc.sync.dma_start(out=page_rows[h][:], in_=pages_by_place[:, :, h * HALF : (h + 1) * HALF])
         nc.sync.dma_start(out=q_rows[:], in_=query.rearrange("(p t) q -> p t q", t=PACK))
+        nc.sync.dma_start(out=key_words[:].bitcast(I32), in_=keys_words[0].bitcast(I32))
         nc.sync.dma_start(page_list[:], offs2)
         for j in range(PACK):
             nc.sync.dma_start(out=val_rows[j][:], in_=vals_by_plane[:, j, :])
@@ -125,21 +126,20 @@ def tile_attend_widelarger_read_lean_pl_kernel(
                 product(nc, h0_bank[:], q2_codes[:, group(g)], q2_scales[:, group(g)], codes[:].bitcast(E4M3X4), scales[:])
                 nc.scalar.copy(out=h0[g][:, first_page : first_page + width], in_=h0_bank[:])
 
-        first_half = quantize_pages("pages0", page_rows[0][:])
         listed_bytes = tile("listed_bytes", [P, I], U8)
         nc.vector.tensor_copy(listed_bytes[:], key_bytes[:].indirect(tokens[:]))
         q2_woven = tile("q2_woven", [P, Q, PACK], BF16)
         weave(nc.scalar.copy, q2_woven[:], q2_rows[:])
-        q2_codes, q2_scales = quantized("q2", q2_woven)
-        score_pages(first_half, 0, 0)
-        listed_words = tile("listed_words", [P, I], U16, "q2_woven")
-        nc.vector.tensor_copy(listed_words[:], key_words[:].indirect(tokens[:]))
+        q2_codes, q2_scales = quantized("q2", q2_woven, "key_bytes")
+        score_pages(quantize_pages("pages0", page_rows[0][:]), 0, 0)
         quarter = HALF // 2
         score_pages(quantize_pages("pages1", page_rows[1][:, :, :quarter]), HALF, 2)
         score_pages(quantize_pages("pages2", page_rows[1][:, :, quarter:]), HALF + quarter, 0)
 
         q_woven = tile("q_woven", [P, Q, PACK], BF16, "pages2_woven")
         weave(nc.vector.tensor_copy, q_woven[:], q_rows[:])
+        listed_words = tile("listed_words", [P, I], U16, "q_rows")
+        nc.vector.tensor_copy(listed_words[:], key_words[:].indirect(tokens[:]))
         q_codes, q_scales = quantized("q", q_woven)
         a_banks = [bank(4 + g, [P, I]) for g in range(GROUPS)]
         for g in range(GROUPS):
@@ -152,10 +152,28 @@ def tile_attend_widelarger_read_lean_pl_kernel(
             nc.tensor.transpose(factor_bank[:, t, :], factor[:, t : t + 1].to_broadcast([P, P]), ident[:])
 
         looked = [tile("looked%d" % g, [P, I], F32) for g in range(GROUPS)]
-        middle = I // 2
         nc.vector.tensor_copy(looked[0][:], h0[0][:].indirect(page_list[:]))
-        nc.scalar.activation(looked[1][:, middle:], h0[1][:].indirect(page_list[:, middle // PER_COLUMN :]), COPY)
-        nc.vector.tensor_copy(looked[1][:, :middle], h0[1][:].indirect(page_list[:, : middle // PER_COLUMN]))
+        nc.scalar.activation(looked[1][:], h0[1][:].indirect(page_list[:]), COPY)
+
+        scores = [tile("scores%d" % g, [P, I], F32) for g in range(GROUPS)]
+        for g in range(GROUPS):
+            nc.vector.scalar_tensor_tensor(
+                out=scores[g][:], in0=a_banks[g][:], scalar=0.0, in1=looked[g][:], op0=ALU.max, op1=ALU.max
+            )
+        weights = [tile("weights%d" % g, [P, I], BF16) for g in range(GROUPS)]
+        w_banks = [bank(g, [P, 2, P]) for g in range(GROUPS)]
+        for g in range(GROUPS):
+            nc.vector.tensor_tensor(
+                out=weights[g][:].rearrange("q (m t) -> q m t", t=PACK),
+                in0=scores[g][:].rearrange("q (m t) -> q m t", t=PACK),
+                in1=factor_bank[:].rearrange("q t m -> q m t"),
+                op=ALU.mult,
+            )
+            turn_pairs(nc, w_banks[g][:], weights[g][:], ident[:])
+        w_woven = tile("w_woven", [P, Q, PACK], BF16)
+        for g in range(GROUPS):
+            weave_pairs(nc.vector.tensor_copy, w_woven[:, group(g), :], w_banks[g][:])
+        w_codes, w_scales = quantized("w", w_woven)
 
         def pick_values(j, tag=None):
             picked = tile("picked%d" % j, [P, I], BF16, tag)
@@ -172,71 +190,43 @@ def tile_attend_widelarger_read_lean_pl_kernel(
             weave_pairs(nc.scalar.copy, woven[:], v_bank[:])
             return woven
 
-        v_bank0 = turn_values(pick_values(0), 6)
-
-        scores = [tile("scores%d" % g, [P, I], F32) for g in range(GROUPS)]
-        for g in range(GROUPS):
-            nc.vector.scalar_tensor_tensor(
-                out=scores[g][:], in0=a_banks[g][:], scalar=0.0, in1=looked[g][:], op0=ALU.max, op1=ALU.max
-            )
-        weights = [tile("weights0", [P, I], BF16, "picked0"), tile("weights1", [P, I], BF16)]
-        w_banks = [bank(g, [P, 2, P]) for g in range(GROUPS)]
-        for g in range(GROUPS):
-            nc.vector.tensor_tensor(
-                out=weights[g][:].rearrange("q (m t) -> q m t", t=PACK),
-                in0=scores[g][:].rearrange("q (m t) -> q m t", t=PACK),
-                in1=factor_bank[:].rearrange("q t m -> q m t"),
-                op=ALU.mult,
-            )
-            turn_pairs(nc, w_banks[g][:], weights[g][:], ident[:])
-        w_woven = tile("w_woven", [P, Q, PACK], BF16)
-        for g in range(GROUPS):
-            weave_pairs(nc.vector.tensor_copy, w_woven[:, group(g), :], w_banks[g][:])
-        w_codes, w_scales = quantized("w", w_woven)
-
-        picked1 = pick_values(1, "val_rows0")
-        picked2 = pick_values(2)
-        v_operands = [quantized("v0", weave_values(0, v_bank0, "val_rows1"), "w_woven")]
-        v_operands.append(quantized("v1", weave_values(1, turn_values(picked1, 2), "val_rows2")))
-        v_woven2 = weave_values(2, turn_values(picked2, 6))
+        picked = [pick_values(0, "h0_1"), pick_values(1, "val_rows0"), pick_values(2)]
+        v_operands = [quantized("v0", weave_values(0, turn_values(picked[0], 6), "val_rows1"), "w_woven")]
+        v_operands.append(quantized("v1", weave_values(1, turn_values(picked[1], 2), "val_rows2")))
+        v_woven2 = weave_values(2, turn_values(picked[2], 6))
 
         out_by_plane = out_0.rearrange("(p j) q -> p j q", j=PACK)
-        o_banks = [bank(6, [P, PACK, P]), bank(3, [P, PACK, P])]
 
-        def multiply(j):
-            codes, scales = v_operands[j]
-            for g in range(GROUPS):
-                product(
-                    nc, o_banks[g][:, j, :], codes[:], scales[:], w_codes[:, group(g)].bitcast(E4M3X4), w_scales[:, group(g)]
-                )
+        def multiply(first, end, number):
+            o_bank = bank(number, [P, end - first, Q])
+            for j in range(first, end):
+                codes, scales = v_operands[j]
+                product(nc, o_bank[:, j - first, :], codes[:], scales[:], w_codes[:].bitcast(E4M3X4), w_scales[:])
+            return o_bank
 
-        def store_planes(first, end, copy, queue, tag=None):
-            result = tile("result%d" % first, [P, end - first, Q], F32, tag)
-            for g in reversed(range(GROUPS)):
-                copy(out=result[:, :, group(g)], in_=o_banks[g][:, first:end, :])
-            queue.dma_start(out=out_by_plane[:, first:end, :], in_=result[:])
+        def store_planes(first, end, o_bank, copy):
+            copy(out=result[:, first:end, :], in_=o_bank[:])
+            nc.sync.dma_start(out=out_by_plane[:, first:end, :], in_=result[:, first:end, :])
 
-        multiply(0)
-        multiply(1)
+        o_bank01 = multiply(0, 2, 6)
 
         last = PACK - 1
-        picked3 = tile("picked3", [P, I], BF16)
+        picked_last = tile("picked_last", [P, I], BF16)
         share = VECTOR_SHARE * PER_COLUMN
-        nc.vector.tensor_copy(picked3[:, :share], val_rows[last][:].indirect(tokens[:, :VECTOR_SHARE]))
-        nc.scalar.activation(picked3[:, share:], val_rows[last][:].indirect(tokens[:, VECTOR_SHARE:]), COPY)
-        v_woven3 = weave_values(last, turn_values(picked3, 7))
-        v_operands.append(quantized("v2", v_woven2, "val_rows3"))
-        store_planes(0, 2, nc.vector.tensor_copy, nc.sync, "v_woven2")
-        multiply(2)
-        v_operands.append(quantized("v3", v_woven3))
-        store_planes(2, last, nc.scalar.copy, nc.sync)
-        multiply(last)
+        nc.vector.tensor_copy(picked_last[:, :share], val_rows[last][:].indirect(tokens[:, :VECTOR_SHARE]))
+        nc.scalar.activation(picked_last[:, share:], val_rows[last][:].indirect(tokens[:, VECTOR_SHARE:]), COPY)
+        v_woven_last = weave_values(last, turn_values(picked_last, 7))
+        result = tile("result", [P, PACK, Q], F32, "val_rows3")
+        store_planes(0, 2, o_bank01, nc.vector.tensor_copy)
+        v_operands.append(quantized("v2", v_woven2, "picked_last"))
+        v_operands.append(quantized("v3", v_woven_last))
+        store_planes(2, last, multiply(2, last, 7), nc.vector.tensor_copy)
+        store_planes(last, PACK, multiply(last, PACK, 2), nc.scalar.copy)
 
         o_woven = tile("o_woven", [P, Q, PACK], BF16)
-        for g, copy in enumerate((nc.vector.tensor_copy, nc.scalar.copy)):
-            copy(out=o_woven[:, group(g), :], in_=o_banks[g][:].rearrange("p j q -> p q j"))
+        weave(nc.vector.tensor_copy, o_woven[:, :OUT_SHARE, :], result[:, :, :OUT_SHARE])
+        weave(nc.scalar.copy, o_woven[:, OUT_SHARE:, :], result[:, :, OUT_SHARE:])
         o_codes, o_scales = quantized("o", o_woven)
-        store_planes(last, PACK, nc.scalar.copy, nc.scalar)
         nc.sync.dma_start(out=out_1[0].rearrange("p c r -> p (c r)").bitcast(I32), in_=o_codes[:].bitcast(I32))
         for quad in range(QUADS):
             queue = nc.sync if quad < QUADS // 2 else nc.scalar

@@ -113,10 +113,10 @@ def tile_attend_widelarger_read_lean_pl_kernel(
 
         h0 = [tile("h0_%d" % g, [P, Z], F32) for g in range(GROUPS)]
 
-        def quantize_pages(name, rows):
+        def weave_pages(name, rows):
             woven = tile(name + "_woven", [P, rows.shape[2], PACK], BF16)
             weave(nc.vector.tensor_copy, woven[:], rows)
-            return quantized(name, woven)
+            return woven
 
         def score_pages(operand, first_page, first_bank):
             codes, scales = operand
@@ -131,16 +131,18 @@ def tile_attend_widelarger_read_lean_pl_kernel(
         q2_woven = tile("q2_woven", [P, Q, PACK], BF16)
         weave(nc.scalar.copy, q2_woven[:], q2_rows[:])
         q2_codes, q2_scales = quantized("q2", q2_woven, "key_bytes")
-        score_pages(quantize_pages("pages0", page_rows[0][:]), 0, 0)
+        score_pages(quantized("pages0", weave_pages("pages0", page_rows[0][:])), 0, 0)
         quarter = HALF // 2
-        score_pages(quantize_pages("pages1", page_rows[1][:, :, :quarter]), HALF, 2)
-        score_pages(quantize_pages("pages2", page_rows[1][:, :, quarter:]), HALF + quarter, 0)
+        third_quarter = weave_pages("pages1", page_rows[1][:, :, :quarter])
+        last_quarter = weave_pages("pages2", page_rows[1][:, :, quarter:])
+        score_pages(quantized("pages1", third_quarter), HALF, 2)
+        score_pages(quantized("pages2", last_quarter), HALF + quarter, 0)
 
         q_woven = tile("q_woven", [P, Q, PACK], BF16, "pages2_woven")
         weave(nc.vector.tensor_copy, q_woven[:], q_rows[:])
+        q_codes, q_scales = quantized("q", q_woven)
         listed_words = tile("listed_words", [P, I], U16, "q_rows")
         nc.vector.tensor_copy(listed_words[:], key_words[:].indirect(tokens[:]))
-        q_codes, q_scales = quantized("q", q_woven)
         a_banks = [bank(4 + g, [P, I]) for g in range(GROUPS)]
         for g in range(GROUPS):
             product(
@@ -152,8 +154,8 @@ def tile_attend_widelarger_read_lean_pl_kernel(
             nc.tensor.transpose(factor_bank[:, t, :], factor[:, t : t + 1].to_broadcast([P, P]), ident[:])
 
         looked = [tile("looked%d" % g, [P, I], F32) for g in range(GROUPS)]
-        nc.vector.tensor_copy(looked[0][:], h0[0][:].indirect(page_list[:]))
-        nc.scalar.activation(looked[1][:], h0[1][:].indirect(page_list[:]), COPY)
+        for g in range(GROUPS):
+            nc.scalar.activation(looked[g][:], h0[g][:].indirect(page_list[:]), COPY)
 
         scores = [tile("scores%d" % g, [P, I], F32) for g in range(GROUPS)]
         for g in range(GROUPS):

from contextlib import ExitStack

import concourse.mybir as mybir
from concourse.masks import make_identity

D, T, I, Q, E, Z = 512, 2048, 512, 256, 512, 1024
FLOPS = 2 * D * Q * I + 2 * D * Q * Z + 2 * I * E * Q

F32 = mybir.dt.float32
BF16 = mybir.dt.bfloat16
I32 = mybir.dt.int32
U32 = mybir.dt.uint32
U16 = mybir.dt.uint16
U8 = mybir.dt.uint8
E4M3X4 = mybir.dt.float8_e4m3fn_x4
E2M1X4 = mybir.dt.float4_e2m1fn_x4
ALU = mybir.AluOpType
COPY = mybir.ActivationFunctionType.Copy

P = 128
PACK = 4
GROUPS = Q // P
QUADS = 4
HALF = Z // 2
RUN = 4
PER_COLUMN = 16
VECTOR_SHARE = 20
OUT_SHARE = 160


def weave(copy, woven, rows):
    copy(
        out=woven.rearrange("p (c i) t -> p c t i", i=RUN),
        in_=rows.rearrange("p t (c i) -> p c t i", i=RUN),
    )


def quantize(nc, codes, scales, woven):
    nc.vector.quantize_mx(out=codes.bitcast(E4M3X4), scales=scales, in_=woven.rearrange("p c t -> p (c t)"))


def product(nc, out, codes, scales, moving, moving_scales):
    nc.tensor.matmul_mx(
        out=out, lhsT=codes.bitcast(E4M3X4), lhsT_scale=scales, rhs=moving, rhs_scale=moving_scales, start=True, stop=True
    )


def turn_pairs(nc, bank, slots, ident):
    pairs = slots.bitcast(F32)
    for u in range(2):
        nc.tensor.transpose(bank[:, u, :], pairs[:, u::2], ident)


def weave_pairs(copy, woven, bank):
    copy(out=woven.bitcast(F32), in_=bank.rearrange("p u c -> p c u"))


def tile_attend_widelarger_read_lean_pl_kernel(
    tc, query, query2, keys_words, keys_scales, pages, slot_factor, vals, offs, offs2, out_0, out_1, out_2
):
    nc = tc.nc
    with ExitStack() as ctx:
        sb = ctx.enter_context(tc.tile_pool(name="sb", bufs=1))
        ps = ctx.enter_context(tc.psum_pool(name="ps", bufs=1))

        def tile(name, shape, dtype, tag=None):
            return sb.tile(shape, dtype, name=name, tag=tag or name, align_bytes=64)

        def bank(number, shape):
            return ps.tile(shape, F32, name="bank%d" % number, tag="bank%d" % number)

        def quantized(name, woven, tag=None):
            width = woven.shape[1]
            codes = tile(name + "_codes", [P, width], U32, tag)
            scales = tile(name + "_scales", [P, width], U8)
            quantize(nc, codes[:], scales[:], woven[:])
            return codes, scales

        def group(g):
            return slice(g * P, (g + 1) * P)

        tokens = sb.tile([P, I // PER_COLUMN], U16, name="tokens")
        page_list = sb.tile([P, I // PER_COLUMN], U16, name="page_list")
        key_words = tile("key_words", [P, T], U16)
        key_bytes = tile("key_bytes", [P, T], U8)
        q_rows = tile("q_rows", [P, PACK, Q], F32)
        q2_rows = tile("q2_rows", [P, PACK, Q], F32)
        page_rows = [tile("page_rows%d" % h, [P, PACK, HALF], F32) for h in range(2)]
        val_rows = [tile("val_rows%d" % j, [P, T], F32) for j in range(PACK)]
        factor = tile("factor", [P, PACK], F32)
        ident = tile("ident", [P, P], F32)

        nc.gpsimd.memset(key_bytes[:].bitcast(I32), 0)
        make_identity(nc, ident[:])

        pages_by_place = pages.rearrange("(p t) z -> p t z", t=PACK)
        vals_by_plane = vals.rearrange("(p j) c -> p j c", j=PACK)
        nc.sync.dma_start(out=q2_rows[:], in_=query2.rearrange("(p t) q -> p t q", t=PACK))
        nc.sync.dma_start(tokens[:], offs)
        nc.sync.dma_start(out=factor[:], in_=slot_factor[0].rearrange("(p t) -> p t", t=PACK))
        for quad in range(QUADS):
            nc.sync.dma_start(
                out=key_bytes[32 * quad : 32 * quad + 4, :].bitcast(I32),
                in_=keys_scales[0][4 * quad : 4 * quad + 4, :].bitcast(I32),
            )
        for h in range(2):
            nc.sync.dma_start(out=page_rows[h][:], in_=pages_by_place[:, :, h * HALF : (h + 1) * HALF])
        nc.sync.dma_start(out=q_rows[:], in_=query.rearrange("(p t) q -> p t q", t=PACK))
        nc.sync.dma_start(out=key_words[:].bitcast(I32), in_=keys_words[0].bitcast(I32))
        nc.sync.dma_start(page_list[:], offs2)
        for j in range(PACK):
            nc.sync.dma_start(out=val_rows[j][:], in_=vals_by_plane[:, j, :])

        h0 = [tile("h0_%d" % g, [P, Z], F32) for g in range(GROUPS)]

        def weave_pages(name, rows):
            woven = tile(name + "_woven", [P, rows.shape[2], PACK], BF16)
            weave(nc.vector.tensor_copy, woven[:], rows)
            return woven

        def score_pages(operand, first_page, first_bank):
            codes, scales = operand
            width = codes.shape[1]
            for g in range(GROUPS):
                h0_bank = bank(first_bank + g, [P, width])
                product(nc, h0_bank[:], q2_codes[:, group(g)], q2_scales[:, group(g)], codes[:].bitcast(E4M3X4), scales[:])
                nc.scalar.copy(out=h0[g][:, first_page : first_page + width], in_=h0_bank[:])

        listed_bytes = tile("listed_bytes", [P, I], U8)
        nc.vector.tensor_copy(listed_bytes[:], key_bytes[:].indirect(tokens[:]))
        q2_woven = tile("q2_woven", [P, Q, PACK], BF16)
        weave(nc.scalar.copy, q2_woven[:], q2_rows[:])
        q2_codes, q2_scales = quantized("q2", q2_woven, "key_bytes")
        score_pages(quantized("pages0", weave_pages("pages0", page_rows[0][:])), 0, 0)
        quarter = HALF // 2
        third_quarter = weave_pages("pages1", page_rows[1][:, :, :quarter])
        last_quarter = weave_pages("pages2", page_rows[1][:, :, quarter:])
        score_pages(quantized("pages1", third_quarter), HALF, 2)
        score_pages(quantized("pages2", last_quarter), HALF + quarter, 0)

        q_woven = tile("q_woven", [P, Q, PACK], BF16, "pages2_woven")
        weave(nc.vector.tensor_copy, q_woven[:], q_rows[:])
        q_codes, q_scales = quantized("q", q_woven)
        listed_words = tile("listed_words", [P, I], U16, "q_rows")
        nc.vector.tensor_copy(listed_words[:], key_words[:].indirect(tokens[:]))
        a_banks = [bank(4 + g, [P, I]) for g in range(GROUPS)]
        for g in range(GROUPS):
            product(
                nc, a_banks[g][:], q_codes[:, group(g)], q_scales[:, group(g)], listed_words[:].bitcast(E2M1X4), listed_bytes[:]
            )

        factor_bank = bank(7, [P, PACK, P])
        for t in range(PACK):
            nc.tensor.transpose(factor_bank[:, t, :], factor[:, t : t + 1].to_broadcast([P, P]), ident[:])

        looked = [tile("looked%d" % g, [P, I], F32) for g in range(GROUPS)]
        for g in range(GROUPS):
            nc.scalar.activation(looked[g][:], h0[g][:].indirect(page_list[:]), COPY)

        scores = [tile("scores%d" % g, [P, I], F32) for g in range(GROUPS)]
        for g in range(GROUPS):
            nc.vector.scalar_tensor_tensor(
                out=scores[g][:], in0=a_banks[g][:], scalar=0.0, in1=looked[g][:], op0=ALU.max, op1=ALU.max
            )
        weights = [tile("weights%d" % g, [P, I], BF16) for g in range(GROUPS)]
        w_banks = [bank(g, [P, 2, P]) for g in range(GROUPS)]
        for g in range(GROUPS):
            nc.vector.tensor_tensor(
                out=weights[g][:].rearrange("q (m t) -> q m t", t=PACK),
                in0=scores[g][:].rearrange("q (m t) -> q m t", t=PACK),
                in1=factor_bank[:].rearrange("q t m -> q m t"),
                op=ALU.mult,
            )
            turn_pairs(nc, w_banks[g][:], weights[g][:], ident[:])
        w_woven = tile("w_woven", [P, Q, PACK], BF16)
        for g in range(GROUPS):
            weave_pairs(nc.vector.tensor_copy, w_woven[:, group(g), :], w_banks[g][:])
        w_codes, w_scales = quantized("w", w_woven)

        def pick_values(j, tag=None):
            picked = tile("picked%d" % j, [P, I], BF16, tag)
            nc.scalar.activation(picked[:], val_rows[j][:].indirect(tokens[:]), COPY)
            return picked

        def turn_values(picked, number):
            v_bank = bank(number, [P, 2, P])
            turn_pairs(nc, v_bank[:], picked[:], ident[:])
            return v_bank

        def weave_values(j, v_bank, tag=None):
            woven = tile("v_woven%d" % j, [P, P, PACK], BF16, tag)
            weave_pairs(nc.scalar.copy, woven[:], v_bank[:])
            return woven

        picked = [pick_values(0, "h0_1"), pick_values(1, "val_rows0"), pick_values(2)]
        v_operands = [quantized("v0", weave_values(0, turn_values(picked[0], 6), "val_rows1"), "w_woven")]
        v_operands.append(quantized("v1", weave_values(1, turn_values(picked[1], 2), "val_rows2")))
        v_woven2 = weave_values(2, turn_values(picked[2], 6))

        out_by_plane = out_0.rearrange("(p j) q -> p j q", j=PACK)

        def multiply(first, end, number):
            o_bank = bank(number, [P, end - first, Q])
            for j in range(first, end):
                codes, scales = v_operands[j]
                product(nc, o_bank[:, j - first, :], codes[:], scales[:], w_codes[:].bitcast(E4M3X4), w_scales[:])
            return o_bank

        def store_planes(first, end, o_bank, copy):
            copy(out=result[:, first:end, :], in_=o_bank[:])
            nc.sync.dma_start(out=out_by_plane[:, first:end, :], in_=result[:, first:end, :])

        o_bank01 = multiply(0, 2, 6)

        last = PACK - 1
        picked_last = tile("picked_last", [P, I], BF16)
        share = VECTOR_SHARE * PER_COLUMN
        nc.vector.tensor_copy(picked_last[:, :share], val_rows[last][:].indirect(tokens[:, :VECTOR_SHARE]))
        nc.scalar.activation(picked_last[:, share:], val_rows[last][:].indirect(tokens[:, VECTOR_SHARE:]), COPY)
        v_woven_last = weave_values(last, turn_values(picked_last, 7))
        result = tile("result", [P, PACK, Q], F32, "val_rows3")
        store_planes(0, 2, o_bank01, nc.vector.tensor_copy)
        v_operands.append(quantized("v2", v_woven2, "picked_last"))
        v_operands.append(quantized("v3", v_woven_last))
        store_planes(2, last, multiply(2, last, 7), nc.vector.tensor_copy)
        store_planes(last, PACK, multiply(last, PACK, 2), nc.scalar.copy)

        o_woven = tile("o_woven", [P, Q, PACK], BF16)
        weave(nc.vector.tensor_copy, o_woven[:, :OUT_SHARE, :], result[:, :, :OUT_SHARE])
        weave(nc.scalar.copy, o_woven[:, OUT_SHARE:, :], result[:, :, OUT_SHARE:])
        o_codes, o_scales = quantized("o", o_woven)
        nc.sync.dma_start(out=out_1[0].rearrange("p c r -> p (c r)").bitcast(I32), in_=o_codes[:].bitcast(I32))
        for quad in range(QUADS):
            queue = nc.sync if quad < QUADS // 2 else nc.scalar
            queue.dma_start(
                out=out_2[0][4 * quad : 4 * quad + 4, :].bitcast(I32),
                in_=o_scales[32 * quad : 32 * quad + 4, :].bitcast(I32),
            )
